import numpy as np
import ml_dtypes


def mxq(x, axis, fmt="e4m3"):
    dtype, down = {"e4m3": (ml_dtypes.float8_e4m3fn, 7), "e5m2": (ml_dtypes.float8_e5m2, 14)}[fmt]
    v = np.moveaxis(np.asarray(x, np.float32).astype(ml_dtypes.bfloat16).astype(np.float64), axis, -1)
    blocks = v.reshape(v.shape[:-1] + (-1, 32))
    amax = np.abs(blocks).max(-1, keepdims=True)
    byte = np.maximum(np.where(amax > 0, np.frexp(amax)[1] - 1 + 127, 0) - down, 1)
    scale = np.exp2(byte - 127.0)
    codes = (blocks / scale).astype(np.float32).astype(dtype).astype(np.float64)
    return np.moveaxis((codes * scale).reshape(v.shape), -1, axis)


WIDE = False


def mx_kscale(k):
    if not WIDE:
        return np.ones(k)
    levels = np.array([10, -10, 5, -5, 0])
    if k % 512:
        return np.exp2(np.random.permutation(np.resize(levels, k // 32))).repeat(32)
    a = np.empty((k // 512, 16))
    for p in range(k // 512):
        a[p, :8] = np.random.permutation(np.resize(levels, 8))
        for g in range(8):
            far = levels[np.abs(levels - a[p, g]) >= 10]
            a[p, g + 8] = far[np.random.randint(len(far))]
    return np.exp2(a.ravel()).repeat(32)


def f64(x):
    return np.asarray(x).astype(np.float64)


def striped(idx):
    return np.tile(idx.reshape(-1, 16).T, (8, 1)).astype(np.uint16)


def unstriped(offs):
    return offs[:16].T.reshape(-1).astype(np.int64)


def striped8(idx):
    return np.concatenate([x.reshape(-1, 16).T for x in idx]).astype(np.uint16)


def runs(offs, k):
    lists = np.stack([offs[16 * r : 16 * r + 16].T.reshape(-1) for r in range(8)]).astype(np.int64)
    return lists[np.arange(k) % 512 // 64]


def pack_weight(w):
    k, n = w.shape
    w = f64(np.asarray(w, np.float32).astype(ml_dtypes.bfloat16)).reshape(k // 32, 32, n)
    amax = np.abs(w).max(1)
    byte = np.clip(np.where(amax > 0, np.frexp(amax)[1] - 1 + 127 - 7, 1), 1, 254)
    scaled = (w * np.exp2(127.0 - byte)[:, None, :]).reshape(k, n).astype(np.float32)
    words = np.ascontiguousarray(scaled.reshape(k // 512, 128, 4, n).transpose(0, 1, 3, 2)).astype(ml_dtypes.float8_e4m3fn).view(np.uint8)
    return words, np.ascontiguousarray(byte.astype(np.uint8).reshape(k // 512, 16, n))


def unpack_weight(words, scales):
    g, p, n, _ = words.shape
    vals = np.ascontiguousarray(words).view(ml_dtypes.float8_e4m3fn).astype(np.float64) * np.repeat(np.exp2(scales.astype(np.float64) - 127.0), 8, axis=1)[..., None]
    return vals.transpose(0, 1, 3, 2).reshape(g * 512, n)


K, T, S, H, C = 512, 2048, 512, 512, 512


def setup_inputs():
    n = np.random.standard_normal
    s = mx_kscale(K)[:, None]
    packed_xT = pack_weight(n((K, T)) * s)
    return {
        "x_words": packed_xT[0],
        "x_scales": packed_xT[1],
        "w1": (n((K, H)) / np.sqrt(K) / s).astype(np.float32),
        "gs": (np.random.uniform(0.5, 1.5, (K, 1)) / s).astype(np.float32),
        "offs": striped(np.random.permutation(T)[:S]),
        "n1": striped8(np.stack([np.random.permutation(S) for _ in range(8)])),
        "n2": striped8(np.stack([np.random.permutation(S) for _ in range(8)])),
        "cand": striped(np.random.permutation(T)[:C]),
        "n3": striped8(np.stack([np.random.permutation(S) for _ in range(8)])),
        "n4": striped8(np.stack([np.random.permutation(S) for _ in range(8)])),
        "n5": striped8(np.stack([np.random.permutation(S) for _ in range(8)])),
    }


def reference(x_words, x_scales, w1, gs, offs, n1, n2, cand, n3, n4, n5):
    x_cand = unpack_weight(x_words, x_scales)[:, unstriped(cand)]
    xq = unpack_weight(x_words, x_scales)[:, unstriped(offs)]
    y = mxq(f64(w1), 0, "e4m3").T @ xq
    ex = np.exp(y)
    z = f64(gs) * (np.log(ex + ex[np.arange(H)[:, None], runs(n1, H)]) - (y[np.arange(H)[:, None], runs(n2, H)]))
    s = 0.0625 * ((x_cand.T @ mxq(z, 0, "e4m3")))
    return np.maximum(s, s[np.arange(C)[:, None], runs(n3, C)]) - (np.maximum(s[np.arange(C)[:, None], runs(n4, C)], s[np.arange(C)[:, None], runs(n5, C)]))

@@ -1,0 +1,218 @@
+from contextlib import ExitStack
+
+import concourse.mybir as mybir
+
+K, T, S, H, C = 512, 2048, 512, 512, 512
+FLOPS = 2 * K * H * S + 2 * H * C * S
+
+F32 = mybir.dt.float32
+BF16 = mybir.dt.bfloat16
+I32 = mybir.dt.int32
+U32 = mybir.dt.uint32
+U16 = mybir.dt.uint16
+U8 = mybir.dt.uint8
+FP8X4 = mybir.dt.float8_e4m3fn_x4
+ALU = mybir.AluOpType
+ACT = mybir.ActivationFunctionType
+
+P = 128
+PACK = 4
+HALF = S // 2
+WINDOW = 2 * S
+LIST_COLS = S // 16
+
+
+def tile_picked_candlsemix_none_p_kernel(
+    tc, x_words, x_scales, w1, gs, offs, n1, n2, cand, n3, n4, n5, out
+):
+    nc = tc.nc
+    planes = range(PACK)
+    halves = range(2)
+
+    with ExitStack() as ctx:
+        keep = ctx.enter_context(tc.tile_pool(name="keep", bufs=1))
+        psum = ctx.enter_context(tc.psum_pool(name="psum", bufs=1))
+
+        def load_list(name, dram):
+            tile = keep.tile([P, LIST_COLS], U16, name=name)
+            nc.sync.dma_start(tile[:], dram)
+            return tile
+
+        table_scales = keep.tile([P, T], U8, name="table_scales")
+        nc.gpsimd.memset(table_scales[:, : T // 2].bitcast(I32), 0)
+        nc.vector.memset(table_scales[:, T // 2 :].bitcast(I32), 0)
+        offs_list = load_list("offs_list", offs)
+        cand_list = load_list("cand_list", cand)
+        gain = keep.tile([P, PACK], F32, name="gain")
+        nc.sync.dma_start(gain[:], gs.rearrange("(p t) o -> p (t o)", t=PACK))
+        for q in range(4):
+            nc.sync.dma_start(
+                table_scales[32 * q : 32 * q + 4, :].bitcast(I32),
+                x_scales[0, 4 * q : 4 * q + 4, :].bitcast(I32),
+            )
+        w_rows = w1.rearrange("(p j) c -> p j c", j=PACK)
+        w_raw = [keep.tile([P, PACK, H // 2], F32, name="w_raw%d" % h) for h in halves]
+        for h in halves:
+            nc.sync.dma_start(w_raw[h][:], w_rows[:, :, h * (H // 2) : (h + 1) * (H // 2)])
+        table_words = keep.tile([P, T], U32, name="table_words")
+        nc.sync.dma_start(
+            table_words[:].bitcast(I32), x_words[0].rearrange("p n t -> p (n t)").bitcast(I32)
+        )
+        n1_list = load_list("n1_list", n1)
+        n2_list = load_list("n2_list", n2)
+        n3_list = load_list("n3_list", n3)
+        n4_list = load_list("n4_list", n4)
+        n5_list = load_list("n5_list", n5)
+
+        first_window = [keep.tile([P, WINDOW], F32, name="first_window%d" % t) for t in planes]
+        y_window = [keep.tile([P, WINDOW], F32, name="y_window%d" % t) for t in planes]
+        for t in planes:
+            nc.vector.memset(first_window[t][:, S:], 0.0)
+
+        tok_words = keep.tile([P, S], U32, name="tok_words", align_bytes=64)
+        tok_scales = keep.tile([P, S], U8, name="tok_scales", align_bytes=64)
+        cand_scales = keep.tile([P, C], U8, name="cand_scales", align_bytes=64)
+        nc.vector.tensor_copy(tok_scales[:], table_scales[:].indirect(offs_list[:]))
+        nc.vector.tensor_copy(cand_scales[:], table_scales[:].indirect(cand_list[:]))
+        dealt_scales = keep.tile([P, C], U8, name="dealt_scales", align_bytes=64)
+        nc.vector.tensor_copy(
+            dealt_scales[:].rearrange("p (t m) -> p m t", t=PACK),
+            cand_scales[:].rearrange("p (m t) -> p m t", t=PACK),
+        )
+
+        w_grouped = keep.tile([P, PACK * P * PACK], BF16, name="w_grouped", align_bytes=64)
+        w_dealt = w_grouped[:].rearrange("p (t m j) -> p m j t", t=PACK, j=PACK)
+        w_src = [w_raw[h][:].rearrange("p j (m t) -> p m j t", t=PACK) for h in halves]
+        for h in halves:
+            nc.scalar.activation(w_dealt[:, h * (P // 2) : (h + 1) * (P // 2)], w_src[h], ACT.Copy)
+
+        w_codes = keep.tile([P, H], U32, name="w_codes", align_bytes=64)
+        w_scales = keep.tile([P, H], U8, name="w_scales", align_bytes=64)
+        y_bank = [psum.tile([P, S], F32, name="y_bank%d" % t) for t in planes]
+        nc.vector.quantize_mx(out=w_codes[:].bitcast(FP8X4), scales=w_scales[:], in_=w_grouped[:])
+        nc.vector.tensor_copy(tok_words[:], table_words[:].indirect(offs_list[:]))
+        for t in planes:
+            cols = slice(t * P, (t + 1) * P)
+            nc.tensor.matmul_mx(
+                out=y_bank[t][:],
+                lhsT=w_codes[:, cols].bitcast(FP8X4),
+                lhsT_scale=w_scales[:, cols],
+                rhs=tok_words[:].bitcast(FP8X4),
+                rhs_scale=tok_scales[:],
+                start=True,
+                stop=True,
+            )
+
+        dealt_words = keep.tile([P, C], U32, name="dealt_words", align_bytes=64)
+        nc.vector.tensor_copy(
+            dealt_words[:].rearrange("p (t m) -> p m t", t=PACK), table_words[:].indirect(cand_list[:])
+        )
+
+        sums = [keep.tile([P, S], F32, name="sums%d" % t) for t in planes]
+        for t in planes:
+            nc.scalar.activation(first_window[t][:, :S], y_bank[t][:], ACT.Exp)
+        for t in planes:
+            nc.vector.tensor_copy(y_window[t][:, S:], first_window[t][:, :S])
+            if t > 0:
+                nc.vector.tensor_tensor(
+                    sums[t - 1][:], first_window[t - 1][:].indirect(n1_list[:]), y_window[t - 1][:, S:], ALU.add
+                )
+        nc.vector.tensor_tensor(
+            sums[PACK - 1][:], first_window[PACK - 1][:].indirect(n1_list[:]), y_window[PACK - 1][:, S:], ALU.add
+        )
+
+        neg_gain = keep.tile([P, PACK], F32, name="neg_gain")
+        nc.vector.tensor_scalar(neg_gain[:], gain[:], -1.0, None, ALU.mult)
+
+        logs = [keep.tile([P, S], F32, name="logs%d" % t) for t in planes]
+        scaled = [keep.tile([P, S], F32, name="scaled%d" % t) for t in planes]
+        z_planes = [keep.tile([P, PACK, HALF], F32, name="z_planes%d" % h) for h in halves]
+        units = [(h, t) for h in halves for t in planes]
+
+        def copy_y(t):
+            nc.scalar.activation(y_window[t][:, :S], y_bank[t][:], ACT.Copy, scale=neg_gain[:, t : t + 1])
+
+        def take_log(h, t):
+            cols = slice(h * HALF, (h + 1) * HALF)
+            nc.scalar.activation(logs[t][:, cols], sums[t][:, cols], ACT.Ln)
+
+        def finish_z(h, t):
+            cols = slice(h * HALF, (h + 1) * HALF)
+            nc.scalar.activation(scaled[t][:, cols], logs[t][:, cols], ACT.Copy, scale=gain[:, t : t + 1])
+            offsets = n2_list[:, h * (LIST_COLS // 2) : (h + 1) * (LIST_COLS // 2)]
+            nc.vector.tensor_tensor(z_planes[h][:, t, :], y_window[t][:].indirect(offsets), scaled[t][:, cols], ALU.add)
+
+        for u, (h, t) in enumerate(units):
+            take_log(h, t)
+            if u > 0:
+                finish_z(*units[u - 1])
+            if h == 0:
+                copy_y(t)
+        finish_z(*units[-1])
+
+        z_grouped = [keep.tile([P, HALF * PACK], BF16, name="z_grouped%d" % h, align_bytes=64) for h in halves]
+        z_dst = [z_grouped[h][:].rearrange("p (c i t) -> p c t i", i=4, t=PACK) for h in halves]
+        z_src = [z_planes[h][:].rearrange("p t (c i) -> p c t i", i=4) for h in halves]
+        share = 48
+        nc.scalar.activation(z_dst[0][:, :share], z_src[0][:, :share], ACT.Copy)
+        nc.vector.tensor_copy(z_dst[1], z_src[1])
+        nc.vector.tensor_copy(z_dst[0][:, share:], z_src[0][:, share:])
+
+        z_codes = keep.tile([P, S], U32, name="z_codes", align_bytes=64)
+        z_scales = keep.tile([P, S], U8, name="z_scales", align_bytes=64)
+        s_bank = [psum.tile([P, S], F32, name="s_bank%d" % t) for t in planes]
+        for h in (1, 0):
+            cols = slice(h * HALF, (h + 1) * HALF)
+            nc.vector.quantize_mx(out=z_codes[:, cols].bitcast(FP8X4), scales=z_scales[:, cols], in_=z_grouped[h][:])
+            for t in planes:
+                rows = slice(t * P, (t + 1) * P)
+                nc.tensor.matmul_mx(
+                    out=s_bank[t][:, cols],
+                    lhsT=dealt_words[:, rows].bitcast(FP8X4),
+                    lhsT_scale=dealt_scales[:, rows],
+                    rhs=z_codes[:, cols].bitcast(FP8X4),
+                    rhs_scale=z_scales[:, cols],
+                    start=True,
+                    stop=True,
+                )
+            nc.scalar.activation(first_window[0][:, cols], s_bank[0][:, cols], ACT.Copy, scale=-0.0625)
+        for t in range(1, PACK):
+            nc.scalar.activation(first_window[t][:, :S], s_bank[t][:], ACT.Copy, scale=-0.0625)
+
+        out_rows = out.rearrange("(p t) j -> t p j", t=PACK)
+        fetched = [keep.tile([P, S], F32, name="fetched%d" % t) for t in planes]
+        least = [keep.tile([P, S], F32, name="least%d" % t) for t in planes]
+        gap4 = [keep.tile([P, S], F32, name="gap4_%d" % t) for t in planes]
+        gap5 = [keep.tile([P, S], F32, name="gap5_%d" % t) for t in planes]
+        result = [keep.tile([P, S], F32, name="result%d" % t) for t in planes]
+
+        def fetch3(t):
+            nc.vector.tensor_copy(fetched[t][:], first_window[t][:].indirect(n3_list[:]))
+
+        def pair3(t):
+            nc.vector.tensor_tensor(least[t][:], first_window[t][:, :S], fetched[t][:], ALU.min)
+
+        def gap(dst, offsets, t):
+            nc.vector.tensor_tensor(dst[t][:], first_window[t][:].indirect(offsets[:]), least[t][:], ALU.subtract)
+
+        fetch3(0)
+        pair3(0)
+        last = PACK - 1
+        for t in range(last):
+            gap(gap4, n4_list, t)
+            fetch3(t + 1)
+            gap(gap5, n5_list, t)
+            pair3(t + 1)
+            nc.vector.tensor_tensor(result[t][:], gap4[t][:], gap5[t][:], ALU.min)
+            nc.sync.dma_start(out_rows[t], result[t][:])
+        for h in halves:
+            cols = slice(h * HALF, (h + 1) * HALF)
+            entries = slice(h * (LIST_COLS // 2), (h + 1) * (LIST_COLS // 2))
+            for dst, offsets in ((gap4, n4_list), (gap5, n5_list)):
+                nc.vector.tensor_tensor(
+                    dst[last][:, cols], first_window[last][:].indirect(offsets[:, entries]), least[last][:, cols], ALU.subtract
+                )
+        for h in halves:
+            cols = slice(h * HALF, (h + 1) * HALF)
+            nc.vector.tensor_tensor(result[last][:, cols], gap4[last][:, cols], gap5[last][:, cols], ALU.min)
+            nc.sync.dma_start(out_rows[last][:, cols], result[last][:, cols])

@@ -1,6 +1,7 @@
 from contextlib import ExitStack
 
 import concourse.mybir as mybir
+from concourse.masks import make_identity
 
 K, T, S, H, C = 512, 2048, 512, 512, 512
 FLOPS = 2 * K * H * S + 2 * H * C * S
@@ -43,10 +44,8 @@ def tile_picked_candlsemix_none_p_kernel(
         nc.vector.memset(table_scales[:, T // 2 :].bitcast(I32), 0)
         offs_list = load_list("offs_list", offs)
         cand_list = load_list("cand_list", cand)
-        gain = keep.tile([P, PACK], F32, name="gain")
-        nc.sync.dma_start(gain[:], gs.rearrange("(p t) o -> p (t o)", t=PACK))
         for q in range(4):
-            nc.sync.dma_start(
+            (nc.sync, nc.scalar)[q % 2].dma_start(
                 table_scales[32 * q : 32 * q + 4, :].bitcast(I32),
                 x_scales[0, 4 * q : 4 * q + 4, :].bitcast(I32),
             )
@@ -58,6 +57,8 @@ def tile_picked_candlsemix_none_p_kernel(
         nc.sync.dma_start(
             table_words[:].bitcast(I32), x_words[0].rearrange("p n t -> p (n t)").bitcast(I32)
         )
+        gain = keep.tile([P, PACK], F32, name="gain")
+        nc.sync.dma_start(gain[:], gs.rearrange("(p t) o -> p (t o)", t=PACK))
         n1_list = load_list("n1_list", n1)
         n2_list = load_list("n2_list", n2)
         n3_list = load_list("n3_list", n3)
@@ -76,8 +77,8 @@ def tile_picked_candlsemix_none_p_kernel(
         nc.vector.tensor_copy(cand_scales[:], table_scales[:].indirect(cand_list[:]))
         dealt_scales = keep.tile([P, C], U8, name="dealt_scales", align_bytes=64)
         nc.vector.tensor_copy(
-            dealt_scales[:].rearrange("p (t m) -> p m t", t=PACK),
-            cand_scales[:].rearrange("p (m t) -> p m t", t=PACK),
+            dealt_scales[:].bitcast(I32).rearrange("p (t a) -> p a t", t=PACK),
+            cand_scales[:].bitcast(I32).rearrange("p (a t) -> p a t", t=PACK),
         )
 
         w_grouped = keep.tile([P, PACK * P * PACK], BF16, name="w_grouped", align_bytes=64)
@@ -105,7 +106,7 @@ def tile_picked_candlsemix_none_p_kernel(
 
         dealt_words = keep.tile([P, C], U32, name="dealt_words", align_bytes=64)
         nc.vector.tensor_copy(
-            dealt_words[:].rearrange("p (t m) -> p m t", t=PACK), table_words[:].indirect(cand_list[:])
+            dealt_words[:].rearrange("p (t a r) -> p a t r", t=PACK, r=4), table_words[:].indirect(cand_list[:])
         )
 
         sums = [keep.tile([P, S], F32, name="sums%d" % t) for t in planes]
@@ -127,7 +128,7 @@ def tile_picked_candlsemix_none_p_kernel(
         logs = [keep.tile([P, S], F32, name="logs%d" % t) for t in planes]
         scaled = [keep.tile([P, S], F32, name="scaled%d" % t) for t in planes]
         z_planes = [keep.tile([P, PACK, HALF], F32, name="z_planes%d" % h) for h in halves]
-        units = [(h, t) for h in halves for t in planes]
+        units = [(h, t) for pair in ((0, 1), (2, 3)) for h in halves for t in pair]
 
         def copy_y(t):
             nc.scalar.activation(y_window[t][:, :S], y_bank[t][:], ACT.Copy, scale=neg_gain[:, t : t + 1])
@@ -142,26 +143,14 @@ def tile_picked_candlsemix_none_p_kernel(
             offsets = n2_list[:, h * (LIST_COLS // 2) : (h + 1) * (LIST_COLS // 2)]
             nc.vector.tensor_tensor(z_planes[h][:, t, :], y_window[t][:].indirect(offsets), scaled[t][:, cols], ALU.add)
 
-        for u, (h, t) in enumerate(units):
-            take_log(h, t)
-            if u > 0:
-                finish_z(*units[u - 1])
-            if h == 0:
-                copy_y(t)
-        finish_z(*units[-1])
-
         z_grouped = [keep.tile([P, HALF * PACK], BF16, name="z_grouped%d" % h, align_bytes=64) for h in halves]
-        z_dst = [z_grouped[h][:].rearrange("p (c i t) -> p c t i", i=4, t=PACK) for h in halves]
-        z_src = [z_planes[h][:].rearrange("p t (c i) -> p c t i", i=4) for h in halves]
-        share = 48
-        nc.scalar.activation(z_dst[0][:, :share], z_src[0][:, :share], ACT.Copy)
-        nc.vector.tensor_copy(z_dst[1], z_src[1])
-        nc.vector.tensor_copy(z_dst[0][:, share:], z_src[0][:, share:])
-
+        z_dst = [z_grouped[h][:].rearrange("p (c t) -> p c t", t=PACK) for h in halves]
+        z_src = [z_planes[h][:].rearrange("p t c -> p c t") for h in halves]
         z_codes = keep.tile([P, S], U32, name="z_codes", align_bytes=64)
         z_scales = keep.tile([P, S], U8, name="z_scales", align_bytes=64)
         s_bank = [psum.tile([P, S], F32, name="s_bank%d" % t) for t in planes]
-        for h in (1, 0):
+
+        def score(h):
             cols = slice(h * HALF, (h + 1) * HALF)
             nc.vector.quantize_mx(out=z_codes[:, cols].bitcast(FP8X4), scales=z_scales[:, cols], in_=z_grouped[h][:])
             for t in planes:
@@ -175,44 +164,88 @@ def tile_picked_candlsemix_none_p_kernel(
                     start=True,
                     stop=True,
                 )
-            nc.scalar.activation(first_window[0][:, cols], s_bank[0][:, cols], ACT.Copy, scale=-0.0625)
-        for t in range(1, PACK):
-            nc.scalar.activation(first_window[t][:, :S], s_bank[t][:], ACT.Copy, scale=-0.0625)
 
-        out_rows = out.rearrange("(p t) j -> t p j", t=PACK)
-        fetched = [keep.tile([P, S], F32, name="fetched%d" % t) for t in planes]
-        least = [keep.tile([P, S], F32, name="least%d" % t) for t in planes]
-        gap4 = [keep.tile([P, S], F32, name="gap4_%d" % t) for t in planes]
-        gap5 = [keep.tile([P, S], F32, name="gap5_%d" % t) for t in planes]
-        result = [keep.tile([P, S], F32, name="result%d" % t) for t in planes]
+        for u, (h, t) in enumerate(units):
+            take_log(h, t)
+            if u > 0:
+                finish_z(*units[u - 1])
+            if h == 0:
+                copy_y(t)
+            if u == 6:
+                nc.vector.tensor_copy(z_dst[0], z_src[0])
+        finish_z(*units[-1])
+        score(0)
+        share = 128
+        nc.scalar.activation(z_dst[1][:, share:], z_src[1][:, share:], ACT.Copy)
+        nc.vector.tensor_copy(z_dst[1][:, :share], z_src[1][:, :share])
+        nc.scalar.activation(first_window[0][:, :HALF], s_bank[0][:, :HALF], ACT.Copy, scale=0.0625)
+        score(1)
+        nc.scalar.activation(first_window[0][:, HALF:S], s_bank[0][:, HALF:], ACT.Copy, scale=0.0625)
 
-        def fetch3(t):
-            nc.vector.tensor_copy(fetched[t][:], first_window[t][:].indirect(n3_list[:]))
-
-        def pair3(t):
-            nc.vector.tensor_tensor(least[t][:], first_window[t][:, :S], fetched[t][:], ALU.min)
-
-        def gap(dst, offsets, t):
-            nc.vector.tensor_tensor(dst[t][:], first_window[t][:].indirect(offsets[:]), least[t][:], ALU.subtract)
-
-        fetch3(0)
-        pair3(0)
+        out_rows = out.rearrange("(a t r) j -> t a r j", t=PACK, r=4)
         last = PACK - 1
+        identity = keep.tile([P, P], F32, name="identity")
+        make_identity(nc, identity[:])
+
+        def tiles(name, count):
+            return [keep.tile([P, S], F32, name="%s%d" % (name, t)) for t in range(count)]
+
+        negated, at4, over3, over4 = (tiles(name, last) for name in ("negated", "at4_", "over3_", "over4_"))
+        rise3_turned = tiles("rise3_turned", last)
+        result = tiles("result", PACK)
+
+        def add_turned(bank, terms):
+            blocks = [(src, b) for src in terms for b in range(4)]
+            for i, (src, b) in enumerate(blocks):
+                cols = slice(b * P, (b + 1) * P)
+                nc.tensor.matmul(
+                    bank[:, cols], src[:, cols], identity[:], start=(i == 0), stop=(i == len(blocks) - 1), is_transpose=True
+                )
+
+        def window(t):
+            nc.scalar.activation(first_window[t][:, :S], s_bank[t][:], ACT.Copy, scale=0.0625)
+
+        def negate(t):
+            nc.scalar.activation(negated[t][:], s_bank[t][:], ACT.Copy, scale=-0.0625)
+
+        def fetch(t):
+            nc.vector.tensor_copy(at4[t][:], first_window[t][:].indirect(n4_list[:]))
+            nc.vector.tensor_tensor(over3[t][:], first_window[t][:].indirect(n3_list[:]), negated[t][:], ALU.add)
+            nc.vector.tensor_tensor(over4[t][:], first_window[t][:].indirect(n5_list[:]), at4[t][:], ALU.subtract)
+
+        def combine(t):
+            spare_bank = y_bank[t - 1]
+            add_turned(spare_bank, [over3[t]])
+            nc.scalar.activation(rise3_turned[t][:], spare_bank[:], ACT.Relu)
+            rise4 = keep.tile([P, S], F32, name="stage")
+            nc.scalar.activation(rise4[:], over4[t][:], ACT.Relu)
+            add_turned(y_bank[t], [negated[t], at4[t], rise4])
+            rest_turned = keep.tile([P, S], F32, name="stage")
+            nc.scalar.activation(rest_turned[:], y_bank[t][:], ACT.Copy, scale=-1.0)
+            add_turned(s_bank[t], [rise3_turned[t], rest_turned])
+            nc.scalar.copy(result[t][:], s_bank[t][:])
+            nc.scalar.dma_start(out_rows[t], result[t][:])
+
+        negate(0)
+        for t in range(1, last):
+            window(t)
+            negate(t)
+        nc.scalar.activation(first_window[last][:, :S], s_bank[last][:], ACT.Copy, scale=-0.0625)
         for t in range(last):
-            gap(gap4, n4_list, t)
-            fetch3(t + 1)
-            gap(gap5, n5_list, t)
-            pair3(t + 1)
-            nc.vector.tensor_tensor(result[t][:], gap4[t][:], gap5[t][:], ALU.min)
-            nc.sync.dma_start(out_rows[t], result[t][:])
+            fetch(t)
+            combine(t)
+
+        fetched, least, end4, end5 = tiles("end", 4)
+        nc.vector.tensor_copy(fetched[:], first_window[last][:].indirect(n3_list[:]))
+        nc.vector.tensor_tensor(least[:], first_window[last][:, :S], fetched[:], ALU.min)
         for h in halves:
             cols = slice(h * HALF, (h + 1) * HALF)
             entries = slice(h * (LIST_COLS // 2), (h + 1) * (LIST_COLS // 2))
-            for dst, offsets in ((gap4, n4_list), (gap5, n5_list)):
+            for dst, offsets in ((end4, n4_list), (end5, n5_list)):
                 nc.vector.tensor_tensor(
-                    dst[last][:, cols], first_window[last][:].indirect(offsets[:, entries]), least[last][:, cols], ALU.subtract
+                    dst[:, cols], first_window[last][:].indirect(offsets[:, entries]), least[:, cols], ALU.subtract
                 )
         for h in halves:
             cols = slice(h * HALF, (h + 1) * HALF)
-            nc.vector.tensor_tensor(result[last][:, cols], gap4[last][:, cols], gap5[last][:, cols], ALU.min)
-            nc.sync.dma_start(out_rows[last][:, cols], result[last][:, cols])
+            nc.vector.tensor_tensor(result[last][:, cols], end4[:, cols], end5[:, cols], ALU.min)
+            nc.sync.dma_start(out_rows[last][:, :, cols], result[last][:, cols])

@@ -32,6 +32,8 @@ def tile_picked_candlsemix_none_p_kernel(
 
     with ExitStack() as ctx:
         keep = ctx.enter_context(tc.tile_pool(name="keep", bufs=1))
+        ring = ctx.enter_context(tc.tile_pool(name="ring", bufs=1))
+        shared = ctx.enter_context(tc.tile_pool(name="shared", bufs=1))
         psum = ctx.enter_context(tc.psum_pool(name="psum", bufs=1))
 
         def load_list(name, dram):
@@ -70,7 +72,6 @@ def tile_picked_candlsemix_none_p_kernel(
         for t in planes:
             nc.vector.memset(first_window[t][:, S:], 0.0)
 
-        tok_words = keep.tile([P, S], U32, name="tok_words", align_bytes=64)
         tok_scales = keep.tile([P, S], U8, name="tok_scales", align_bytes=64)
         cand_scales = keep.tile([P, C], U8, name="cand_scales", align_bytes=64)
         nc.vector.tensor_copy(tok_scales[:], table_scales[:].indirect(offs_list[:]))
@@ -81,7 +82,7 @@ def tile_picked_candlsemix_none_p_kernel(
             cand_scales[:].bitcast(I32).rearrange("p (a t) -> p a t", t=PACK),
         )
 
-        w_grouped = keep.tile([P, PACK * P * PACK], BF16, name="w_grouped", align_bytes=64)
+        w_grouped = shared.tile([P, PACK * P * PACK], BF16, name="w_grouped", align_bytes=64, offset=0)
         w_dealt = w_grouped[:].rearrange("p (t m j) -> p m j t", t=PACK, j=PACK)
         w_src = [w_raw[h][:].rearrange("p j (m t) -> p m j t", t=PACK) for h in halves]
         for h in halves:
@@ -90,28 +91,44 @@ def tile_picked_candlsemix_none_p_kernel(
         w_codes = keep.tile([P, H], U32, name="w_codes", align_bytes=64)
         w_scales = keep.tile([P, H], U8, name="w_scales", align_bytes=64)
         y_bank = [psum.tile([P, S], F32, name="y_bank%d" % t) for t in planes]
+        s_bank = [psum.tile([P, S], F32, name="s_bank%d" % t) for t in planes]
         nc.vector.quantize_mx(out=w_codes[:].bitcast(FP8X4), scales=w_scales[:], in_=w_grouped[:])
-        nc.vector.tensor_copy(tok_words[:], table_words[:].indirect(offs_list[:]))
-        for t in planes:
-            cols = slice(t * P, (t + 1) * P)
+        tok_words = shared.tile([P, S], U32, name="tok_words", align_bytes=64, offset=0)
+        half_cols = [slice(h * HALF, (h + 1) * HALF) for h in halves]
+        half_list = [slice(h * (LIST_COLS // 2), (h + 1) * (LIST_COLS // 2)) for h in halves]
+        for h in halves:
+            nc.vector.tensor_copy(tok_words[:, half_cols[h]], table_words[:].indirect(offs_list[:, half_list[h]]))
+
+        def product(bank, words, scales, t, moving_words, moving_scales, cols):
+            rows = slice(t * P, (t + 1) * P)
             nc.tensor.matmul_mx(
-                out=y_bank[t][:],
-                lhsT=w_codes[:, cols].bitcast(FP8X4),
-                lhsT_scale=w_scales[:, cols],
-                rhs=tok_words[:].bitcast(FP8X4),
-                rhs_scale=tok_scales[:],
+                out=bank[:, cols],
+                lhsT=words[:, rows].bitcast(FP8X4),
+                lhsT_scale=scales[:, rows],
+                rhs=moving_words[:, cols].bitcast(FP8X4),
+                rhs_scale=moving_scales[:, cols],
                 start=True,
                 stop=True,
             )
 
-        dealt_words = keep.tile([P, C], U32, name="dealt_words", align_bytes=64)
+        def pieces(banks, spare_bank):
+            return [(0, half_cols[0], spare_bank), (0, half_cols[1], banks[0])] + [
+                (t, slice(0, S), banks[t]) for t in range(1, PACK)
+            ]
+
+        y_pieces = pieces(y_bank, s_bank[0])
+        s_pieces = pieces(s_bank, y_bank[0])
+        for t, cols, bank in y_pieces:
+            product(bank, w_codes, w_scales, t, tok_words, tok_scales, cols)
+
+        dealt_words = shared.tile([P, C], U32, name="dealt_words", align_bytes=64, offset=4 * S)
         nc.vector.tensor_copy(
             dealt_words[:].rearrange("p (t a r) -> p a t r", t=PACK, r=4), table_words[:].indirect(cand_list[:])
         )
 
         sums = [keep.tile([P, S], F32, name="sums%d" % t) for t in planes]
-        for t in planes:
-            nc.scalar.activation(first_window[t][:, :S], y_bank[t][:], ACT.Exp)
+        for t, cols, bank in y_pieces:
+            nc.scalar.activation(first_window[t][:, cols], bank[:, cols], ACT.Exp)
         for t in planes:
             nc.vector.tensor_copy(y_window[t][:, S:], first_window[t][:, :S])
             if t > 0:
@@ -123,7 +140,7 @@ def tile_picked_candlsemix_none_p_kernel(
         )
 
         neg_gain = keep.tile([P, PACK], F32, name="neg_gain")
-        nc.vector.tensor_scalar(neg_gain[:], gain[:], -1.0, None, ALU.mult)
+        nc.gpsimd.tensor_scalar(neg_gain[:], gain[:], -1.0, None, ALU.mult)
 
         logs = [keep.tile([P, S], F32, name="logs%d" % t) for t in planes]
         scaled = [keep.tile([P, S], F32, name="scaled%d" % t) for t in planes]
@@ -131,7 +148,9 @@ def tile_picked_candlsemix_none_p_kernel(
         units = [(h, t) for pair in ((0, 1), (2, 3)) for h in halves for t in pair]
 
         def copy_y(t):
-            nc.scalar.activation(y_window[t][:, :S], y_bank[t][:], ACT.Copy, scale=neg_gain[:, t : t + 1])
+            for tile, cols, bank in y_pieces:
+                if tile == t:
+                    nc.scalar.activation(y_window[t][:, cols], bank[:, cols], ACT.Copy, scale=neg_gain[:, t : t + 1])
 
         def take_log(h, t):
             cols = slice(h * HALF, (h + 1) * HALF)
@@ -148,22 +167,6 @@ def tile_picked_candlsemix_none_p_kernel(
         z_src = [z_planes[h][:].rearrange("p t c -> p c t") for h in halves]
         z_codes = keep.tile([P, S], U32, name="z_codes", align_bytes=64)
         z_scales = keep.tile([P, S], U8, name="z_scales", align_bytes=64)
-        s_bank = [psum.tile([P, S], F32, name="s_bank%d" % t) for t in planes]
-
-        def score(h):
-            cols = slice(h * HALF, (h + 1) * HALF)
-            nc.vector.quantize_mx(out=z_codes[:, cols].bitcast(FP8X4), scales=z_scales[:, cols], in_=z_grouped[h][:])
-            for t in planes:
-                rows = slice(t * P, (t + 1) * P)
-                nc.tensor.matmul_mx(
-                    out=s_bank[t][:, cols],
-                    lhsT=dealt_words[:, rows].bitcast(FP8X4),
-                    lhsT_scale=dealt_scales[:, rows],
-                    rhs=z_codes[:, cols].bitcast(FP8X4),
-                    rhs_scale=z_scales[:, cols],
-                    start=True,
-                    stop=True,
-                )
 
         for u, (h, t) in enumerate(units):
             take_log(h, t)
@@ -171,16 +174,15 @@ def tile_picked_candlsemix_none_p_kernel(
                 finish_z(*units[u - 1])
             if h == 0:
                 copy_y(t)
-            if u == 6:
-                nc.vector.tensor_copy(z_dst[0], z_src[0])
         finish_z(*units[-1])
-        score(0)
-        share = 128
-        nc.scalar.activation(z_dst[1][:, share:], z_src[1][:, share:], ACT.Copy)
-        nc.vector.tensor_copy(z_dst[1][:, :share], z_src[1][:, :share])
-        nc.scalar.activation(first_window[0][:, :HALF], s_bank[0][:, :HALF], ACT.Copy, scale=0.0625)
-        score(1)
-        nc.scalar.activation(first_window[0][:, HALF:S], s_bank[0][:, HALF:], ACT.Copy, scale=0.0625)
+        nc.scalar.activation(z_dst[0], z_src[0], ACT.Copy)
+        nc.vector.tensor_copy(z_dst[1], z_src[1])
+        for h in halves:
+            nc.vector.quantize_mx(
+                out=z_codes[:, half_cols[h]].bitcast(FP8X4), scales=z_scales[:, half_cols[h]], in_=z_grouped[h][:]
+            )
+        for t, cols, bank in s_pieces:
+            product(bank, dealt_words, dealt_scales, t, z_codes, z_scales, cols)
 
         out_rows = out.rearrange("(a t r) j -> t a r j", t=PACK, r=4)
         last = PACK - 1
@@ -190,62 +192,85 @@ def tile_picked_candlsemix_none_p_kernel(
         def tiles(name, count):
             return [keep.tile([P, S], F32, name="%s%d" % (name, t)) for t in range(count)]
 
-        negated, at4, over3, over4 = (tiles(name, last) for name in ("negated", "at4_", "over3_", "over4_"))
-        rise3_turned = tiles("rise3_turned", last)
+        plain, drop, rise, least, turned = (tiles(name, last) for name in ("plain", "drop", "rise", "least", "turned"))
         result = tiles("result", PACK)
+        gap4, gap5 = {}, {}
 
-        def add_turned(bank, terms):
-            blocks = [(src, b) for src in terms for b in range(4)]
+        def add_turned(bank, terms, h):
+            blocks = [(src, b) for src in terms for b in (2 * h, 2 * h + 1)]
             for i, (src, b) in enumerate(blocks):
                 cols = slice(b * P, (b + 1) * P)
                 nc.tensor.matmul(
                     bank[:, cols], src[:, cols], identity[:], start=(i == 0), stop=(i == len(blocks) - 1), is_transpose=True
                 )
 
-        def window(t):
-            nc.scalar.activation(first_window[t][:, :S], s_bank[t][:], ACT.Copy, scale=0.0625)
+        def window(t, cols, bank):
+            nc.scalar.activation(first_window[t][:, cols], bank[:, cols], ACT.Copy, scale=-0.0625)
+            if t < last:
+                nc.scalar.activation(plain[t][:, cols], bank[:, cols], ACT.Copy, scale=0.0625)
 
-        def negate(t):
-            nc.scalar.activation(negated[t][:], s_bank[t][:], ACT.Copy, scale=-0.0625)
+        def against3(t, cols, entries):
+            nc.vector.tensor_tensor(drop[t][:, cols], first_window[t][:].indirect(n3_list[:, entries]), plain[t][:, cols], ALU.add)
 
-        def fetch(t):
-            nc.vector.tensor_copy(at4[t][:], first_window[t][:].indirect(n4_list[:]))
-            nc.vector.tensor_tensor(over3[t][:], first_window[t][:].indirect(n3_list[:]), negated[t][:], ALU.add)
-            nc.vector.tensor_tensor(over4[t][:], first_window[t][:].indirect(n5_list[:]), at4[t][:], ALU.subtract)
+        def rectify(t):
+            nc.scalar.activation(rise[t][:], drop[t][:], ACT.Relu, scale=-1.0)
 
-        def combine(t):
-            spare_bank = y_bank[t - 1]
-            add_turned(spare_bank, [over3[t]])
-            nc.scalar.activation(rise3_turned[t][:], spare_bank[:], ACT.Relu)
-            rise4 = keep.tile([P, S], F32, name="stage")
-            nc.scalar.activation(rise4[:], over4[t][:], ACT.Relu)
-            add_turned(y_bank[t], [negated[t], at4[t], rise4])
-            rest_turned = keep.tile([P, S], F32, name="stage")
-            nc.scalar.activation(rest_turned[:], y_bank[t][:], ACT.Copy, scale=-1.0)
-            add_turned(s_bank[t], [rise3_turned[t], rest_turned])
-            nc.scalar.copy(result[t][:], s_bank[t][:])
+        def against4(t):
+            gap4[t] = ring.tile([P, S], F32, name="gap4", bufs=2)
+            nc.vector.tensor_tensor(gap4[t][:], first_window[t][:].indirect(n4_list[:]), rise[t][:], ALU.add)
+
+        def against5(t):
+            gap5[t] = ring.tile([P, S], F32, name="gap5", bufs=1)
+            nc.vector.tensor_tensor(gap5[t][:], first_window[t][:].indirect(n5_list[:]), rise[t][:], ALU.add)
+
+        def add_and_store(t):
+            nc.vector.tensor_tensor(least[t][:], gap4[t][:], gap5[t][:], ALU.min)
+            for h, cols in enumerate(half_cols):
+                add_turned(y_bank[h], [plain[t], least[t]], h)
+                nc.scalar.copy(turned[t][:, cols], y_bank[h][:, cols])
+            for h, cols in enumerate(half_cols):
+                add_turned(y_bank[2 + h], [turned[t]], h)
+                nc.scalar.copy(result[t][:, cols], y_bank[2 + h][:, cols])
             nc.scalar.dma_start(out_rows[t], result[t][:])
 
-        negate(0)
-        for t in range(1, last):
-            window(t)
-            negate(t)
-        nc.scalar.activation(first_window[last][:, :S], s_bank[last][:], ACT.Copy, scale=-0.0625)
-        for t in range(last):
-            fetch(t)
-            combine(t)
-
-        fetched, least, end4, end5 = tiles("end", 4)
-        nc.vector.tensor_copy(fetched[:], first_window[last][:].indirect(n3_list[:]))
-        nc.vector.tensor_tensor(least[:], first_window[last][:, :S], fetched[:], ALU.min)
+        whole, all_entries = slice(0, S), slice(0, LIST_COLS)
         for h in halves:
-            cols = slice(h * HALF, (h + 1) * HALF)
-            entries = slice(h * (LIST_COLS // 2), (h + 1) * (LIST_COLS // 2))
+            window(*s_pieces[h])
+        for h in halves:
+            against3(0, half_cols[h], half_list[h])
+        window(*s_pieces[2])
+        rectify(0)
+        against3(1, whole, all_entries)
+        window(*s_pieces[3])
+        rectify(1)
+        window(*s_pieces[4])
+        against4(0)
+        against5(0)
+        against3(2, whole, all_entries)
+        rectify(2)
+        add_and_store(0)
+        against4(1)
+        against5(1)
+        against4(2)
+        add_and_store(1)
+        against5(2)
+
+        at3 = ring.tile([P, S], F32, name="gap4", bufs=2)
+        lower, end4, end5 = tiles("end", 3)
+
+        def fetch3(h):
+            nc.vector.tensor_copy(at3[:, half_cols[h]], first_window[last][:].indirect(n3_list[:, half_list[h]]))
+
+        fetch3(0)
+        add_and_store(2)
+        fetch3(1)
+        for cols in half_cols:
+            nc.vector.tensor_tensor(lower[:, cols], first_window[last][:, cols], at3[:, cols], ALU.min)
+        for h, cols in enumerate(half_cols):
             for dst, offsets in ((end4, n4_list), (end5, n5_list)):
                 nc.vector.tensor_tensor(
-                    dst[:, cols], first_window[last][:].indirect(offsets[:, entries]), least[:, cols], ALU.subtract
+                    dst[:, cols], first_window[last][:].indirect(offsets[:, half_list[h]]), lower[:, cols], ALU.subtract
                 )
-        for h in halves:
-            cols = slice(h * HALF, (h + 1) * HALF)
+        for cols in half_cols:
             nc.vector.tensor_tensor(result[last][:, cols], end4[:, cols], end5[:, cols], ALU.min)
             nc.sync.dma_start(out_rows[last][:, :, cols], result[last][:, cols])

@@ -163,8 +163,8 @@ def tile_picked_candlsemix_none_p_kernel(
             nc.vector.tensor_tensor(z_planes[h][:, t, :], y_window[t][:].indirect(offsets), scaled[t][:, cols], ALU.add)
 
         z_grouped = [keep.tile([P, HALF * PACK], BF16, name="z_grouped%d" % h, align_bytes=64) for h in halves]
-        z_dst = [z_grouped[h][:].rearrange("p (c t) -> p c t", t=PACK) for h in halves]
-        z_src = [z_planes[h][:].rearrange("p t c -> p c t") for h in halves]
+        z_dst = [z_grouped[h][:].rearrange("p (c i t) -> p c t i", i=4, t=PACK) for h in halves]
+        z_src = [z_planes[h][:].rearrange("p t (c i) -> p c t i", i=4) for h in halves]
         z_codes = keep.tile([P, S], U32, name="z_codes", align_bytes=64)
         z_scales = keep.tile([P, S], U8, name="z_scales", align_bytes=64)
 
@@ -209,8 +209,8 @@ def tile_picked_candlsemix_none_p_kernel(
             if t < last:
                 nc.scalar.activation(plain[t][:, cols], bank[:, cols], ACT.Copy, scale=0.0625)
 
-        def against3(t, cols, entries):
-            nc.vector.tensor_tensor(drop[t][:, cols], first_window[t][:].indirect(n3_list[:, entries]), plain[t][:, cols], ALU.add)
+        def against3(t):
+            nc.vector.tensor_tensor(drop[t][:], first_window[t][:].indirect(n3_list[:]), plain[t][:], ALU.add)
 
         def rectify(t):
             nc.scalar.activation(rise[t][:], drop[t][:], ACT.Relu, scale=-1.0)
@@ -223,36 +223,41 @@ def tile_picked_candlsemix_none_p_kernel(
             gap5[t] = ring.tile([P, S], F32, name="gap5", bufs=1)
             nc.vector.tensor_tensor(gap5[t][:], first_window[t][:].indirect(n5_list[:]), rise[t][:], ALU.add)
 
-        def add_and_store(t):
+        def smaller_gap(t):
             nc.vector.tensor_tensor(least[t][:], gap4[t][:], gap5[t][:], ALU.min)
+            add_and_store(t, [plain[t], least[t]])
+
+        def add_and_store(t, terms):
             for h, cols in enumerate(half_cols):
-                add_turned(y_bank[h], [plain[t], least[t]], h)
+                add_turned(y_bank[h], terms, h)
                 nc.scalar.copy(turned[t][:, cols], y_bank[h][:, cols])
             for h, cols in enumerate(half_cols):
                 add_turned(y_bank[2 + h], [turned[t]], h)
                 nc.scalar.copy(result[t][:, cols], y_bank[2 + h][:, cols])
             nc.scalar.dma_start(out_rows[t], result[t][:])
 
-        whole, all_entries = slice(0, S), slice(0, LIST_COLS)
         for h in halves:
             window(*s_pieces[h])
-        for h in halves:
-            against3(0, half_cols[h], half_list[h])
+        at4, excess, shortfall = tiles("first", 3)
+        step5 = drop[2]
+        nc.vector.tensor_copy(at4[:], first_window[0][:].indirect(n4_list[:]))
+        against3(0)
+        nc.vector.tensor_tensor(step5[:], first_window[0][:].indirect(n5_list[:]), at4[:], ALU.subtract)
         window(*s_pieces[2])
         rectify(0)
-        against3(1, whole, all_entries)
         window(*s_pieces[3])
+        nc.scalar.activation(excess[:], step5[:], ACT.Relu, scale=-1.0)
+        nc.scalar.activation(shortfall[:], excess[:], ACT.Copy, scale=-1.0)
+        against3(1)
         rectify(1)
         window(*s_pieces[4])
-        against4(0)
-        against5(0)
-        against3(2, whole, all_entries)
+        against3(2)
         rectify(2)
-        add_and_store(0)
+        add_and_store(0, [plain[0], at4, rise[0], shortfall])
         against4(1)
         against5(1)
         against4(2)
-        add_and_store(1)
+        smaller_gap(1)
         against5(2)
 
         at3 = ring.tile([P, S], F32, name="gap4", bufs=2)
@@ -262,7 +267,7 @@ def tile_picked_candlsemix_none_p_kernel(
             nc.vector.tensor_copy(at3[:, half_cols[h]], first_window[last][:].indirect(n3_list[:, half_list[h]]))
 
         fetch3(0)
-        add_and_store(2)
+        smaller_gap(2)
         fetch3(1)
         for cols in half_cols:
             nc.vector.tensor_tensor(lower[:, cols], first_window[last][:, cols], at3[:, cols], ALU.min)

@@ -4,7 +4,7 @@ import concourse.mybir as mybir
 from concourse.masks import make_identity
 
 K, T, S, H, C = 512, 2048, 512, 512, 512
-FLOPS = 2 * K * H * S + 2 * H * C * S
+FLOPS = 2 * K * H * S + 2 * K * C * S
 
 F32 = mybir.dt.float32
 BF16 = mybir.dt.bfloat16
@@ -18,17 +18,22 @@ ACT = mybir.ActivationFunctionType
 
 P = 128
 PACK = 4
+LAST = PACK - 1
 HALF = S // 2
 WINDOW = 2 * S
 LIST_COLS = S // 16
+LINE = 4
+SCORE_SCALE = 0.0625
 
 
 def tile_picked_candlsemix_none_p_kernel(
     tc, x_words, x_scales, w1, gs, offs, n1, n2, cand, n3, n4, n5, out
 ):
     nc = tc.nc
-    planes = range(PACK)
+    row_tiles = range(PACK)
     halves = range(2)
+    half_cols = [slice(h * HALF, (h + 1) * HALF) for h in halves]
+    half_list = [slice(h * (LIST_COLS // 2), (h + 1) * (LIST_COLS // 2)) for h in halves]
 
     with ExitStack() as ctx:
         keep = ctx.enter_context(tc.tile_pool(name="keep", bufs=1))
@@ -40,6 +45,9 @@ def tile_picked_candlsemix_none_p_kernel(
             tile = keep.tile([P, LIST_COLS], U16, name=name)
             nc.sync.dma_start(tile[:], dram)
             return tile
+
+        def row_buffers(name, count):
+            return [keep.tile([P, S], F32, name="%s%d" % (name, i)) for i in range(count)]
 
         table_scales = keep.tile([P, T], U8, name="table_scales")
         nc.gpsimd.memset(table_scales[:, : T // 2].bitcast(I32), 0)
@@ -57,7 +65,7 @@ def tile_picked_candlsemix_none_p_kernel(
             nc.sync.dma_start(w_raw[h][:], w_rows[:, :, h * (H // 2) : (h + 1) * (H // 2)])
         table_words = keep.tile([P, T], U32, name="table_words")
         nc.sync.dma_start(
-            table_words[:].bitcast(I32), x_words[0].rearrange("p n t -> p (n t)").bitcast(I32)
+            table_words[:].bitcast(I32), x_words[0].rearrange("p n j -> p (n j)").bitcast(I32)
         )
         gain = keep.tile([P, PACK], F32, name="gain")
         nc.sync.dma_start(gain[:], gs.rearrange("(p t) o -> p (t o)", t=PACK))
@@ -67,10 +75,10 @@ def tile_picked_candlsemix_none_p_kernel(
         n4_list = load_list("n4_list", n4)
         n5_list = load_list("n5_list", n5)
 
-        first_window = [keep.tile([P, WINDOW], F32, name="first_window%d" % t) for t in planes]
-        y_window = [keep.tile([P, WINDOW], F32, name="y_window%d" % t) for t in planes]
-        for t in planes:
-            nc.vector.memset(first_window[t][:, S:], 0.0)
+        window = [keep.tile([P, WINDOW], F32, name="window%d" % t) for t in row_tiles]
+        y_window = [keep.tile([P, WINDOW], F32, name="y_window%d" % t) for t in row_tiles]
+        for t in row_tiles:
+            nc.vector.memset(window[t][:, S:], 0.0)
 
         tok_scales = keep.tile([P, S], U8, name="tok_scales", align_bytes=64)
         cand_scales = keep.tile([P, C], U8, name="cand_scales", align_bytes=64)
@@ -84,18 +92,19 @@ def tile_picked_candlsemix_none_p_kernel(
 
         w_grouped = shared.tile([P, PACK * P * PACK], BF16, name="w_grouped", align_bytes=64, offset=0)
         w_dealt = w_grouped[:].rearrange("p (t m j) -> p m j t", t=PACK, j=PACK)
-        w_src = [w_raw[h][:].rearrange("p j (m t) -> p m j t", t=PACK) for h in halves]
         for h in halves:
-            nc.scalar.activation(w_dealt[:, h * (P // 2) : (h + 1) * (P // 2)], w_src[h], ACT.Copy)
-
+            nc.scalar.activation(
+                w_dealt[:, h * (P // 2) : (h + 1) * (P // 2)],
+                w_raw[h][:].rearrange("p j (m t) -> p m j t", t=PACK),
+                ACT.Copy,
+            )
         w_codes = keep.tile([P, H], U32, name="w_codes", align_bytes=64)
         w_scales = keep.tile([P, H], U8, name="w_scales", align_bytes=64)
-        y_bank = [psum.tile([P, S], F32, name="y_bank%d" % t) for t in planes]
-        s_bank = [psum.tile([P, S], F32, name="s_bank%d" % t) for t in planes]
+        y_bank = [psum.tile([P, S], F32, name="y_bank%d" % t) for t in row_tiles]
+        s_bank = [psum.tile([P, S], F32, name="s_bank%d" % t) for t in row_tiles]
         nc.vector.quantize_mx(out=w_codes[:].bitcast(FP8X4), scales=w_scales[:], in_=w_grouped[:])
+
         tok_words = shared.tile([P, S], U32, name="tok_words", align_bytes=64, offset=0)
-        half_cols = [slice(h * HALF, (h + 1) * HALF) for h in halves]
-        half_list = [slice(h * (LIST_COLS // 2), (h + 1) * (LIST_COLS // 2)) for h in halves]
         for h in halves:
             nc.vector.tensor_copy(tok_words[:, half_cols[h]], table_words[:].indirect(offs_list[:, half_list[h]]))
 
@@ -123,159 +132,140 @@ def tile_picked_candlsemix_none_p_kernel(
 
         dealt_words = shared.tile([P, C], U32, name="dealt_words", align_bytes=64, offset=4 * S)
         nc.vector.tensor_copy(
-            dealt_words[:].rearrange("p (t a r) -> p a t r", t=PACK, r=4), table_words[:].indirect(cand_list[:])
+            dealt_words[:].rearrange("p (t a r) -> p a t r", t=PACK, r=LINE), table_words[:].indirect(cand_list[:])
         )
 
-        sums = [keep.tile([P, S], F32, name="sums%d" % t) for t in planes]
+        sums = row_buffers("sums", PACK)
         for t, cols, bank in y_pieces:
-            nc.scalar.activation(first_window[t][:, cols], bank[:, cols], ACT.Exp)
-        for t in planes:
-            nc.vector.tensor_copy(y_window[t][:, S:], first_window[t][:, :S])
+            nc.scalar.activation(window[t][:, cols], bank[:, cols], ACT.Exp)
+
+        def add_looked_up(t):
+            nc.vector.tensor_tensor(sums[t][:], window[t][:].indirect(n1_list[:]), y_window[t][:, S:], ALU.add)
+
+        for t in row_tiles:
+            nc.vector.tensor_copy(y_window[t][:, S:], window[t][:, :S])
             if t > 0:
-                nc.vector.tensor_tensor(
-                    sums[t - 1][:], first_window[t - 1][:].indirect(n1_list[:]), y_window[t - 1][:, S:], ALU.add
-                )
-        nc.vector.tensor_tensor(
-            sums[PACK - 1][:], first_window[PACK - 1][:].indirect(n1_list[:]), y_window[PACK - 1][:, S:], ALU.add
-        )
+                add_looked_up(t - 1)
+        add_looked_up(LAST)
 
         neg_gain = keep.tile([P, PACK], F32, name="neg_gain")
         nc.gpsimd.tensor_scalar(neg_gain[:], gain[:], -1.0, None, ALU.mult)
-
-        logs = [keep.tile([P, S], F32, name="logs%d" % t) for t in planes]
-        scaled = [keep.tile([P, S], F32, name="scaled%d" % t) for t in planes]
-        z_planes = [keep.tile([P, PACK, HALF], F32, name="z_planes%d" % h) for h in halves]
-        units = [(h, t) for pair in ((0, 1), (2, 3)) for h in halves for t in pair]
-
-        def copy_y(t):
-            for tile, cols, bank in y_pieces:
-                if tile == t:
-                    nc.scalar.activation(y_window[t][:, cols], bank[:, cols], ACT.Copy, scale=neg_gain[:, t : t + 1])
-
-        def take_log(h, t):
-            cols = slice(h * HALF, (h + 1) * HALF)
-            nc.scalar.activation(logs[t][:, cols], sums[t][:, cols], ACT.Ln)
-
-        def finish_z(h, t):
-            cols = slice(h * HALF, (h + 1) * HALF)
-            nc.scalar.activation(scaled[t][:, cols], logs[t][:, cols], ACT.Copy, scale=gain[:, t : t + 1])
-            offsets = n2_list[:, h * (LIST_COLS // 2) : (h + 1) * (LIST_COLS // 2)]
-            nc.vector.tensor_tensor(z_planes[h][:, t, :], y_window[t][:].indirect(offsets), scaled[t][:, cols], ALU.add)
-
+        logs = row_buffers("logs", PACK)
+        weighted_logs = row_buffers("weighted_logs", PACK)
+        z_tiles = [keep.tile([P, PACK, HALF], F32, name="z_tiles%d" % h) for h in halves]
         z_grouped = [keep.tile([P, HALF * PACK], BF16, name="z_grouped%d" % h, align_bytes=64) for h in halves]
-        z_dst = [z_grouped[h][:].rearrange("p (c i t) -> p c t i", i=4, t=PACK) for h in halves]
-        z_src = [z_planes[h][:].rearrange("p t (c i) -> p c t i", i=4) for h in halves]
         z_codes = keep.tile([P, S], U32, name="z_codes", align_bytes=64)
         z_scales = keep.tile([P, S], U8, name="z_scales", align_bytes=64)
 
-        for u, (h, t) in enumerate(units):
+        def fill_y_window(t):
+            for piece_tile, cols, bank in y_pieces:
+                if piece_tile == t:
+                    nc.scalar.activation(y_window[t][:, cols], bank[:, cols], ACT.Copy, scale=neg_gain[:, t : t + 1])
+
+        def take_log(h, t):
+            nc.scalar.activation(logs[t][:, half_cols[h]], sums[t][:, half_cols[h]], ACT.Ln)
+
+        def make_z(h, t):
+            cols = half_cols[h]
+            nc.scalar.activation(weighted_logs[t][:, cols], logs[t][:, cols], ACT.Copy, scale=gain[:, t : t + 1])
+            nc.vector.tensor_tensor(
+                z_tiles[h][:, t, :], y_window[t][:].indirect(n2_list[:, half_list[h]]), weighted_logs[t][:, cols], ALU.add
+            )
+
+        steps = [(h, t) for pair in ((0, 1), (2, 3)) for h in halves for t in pair]
+        for i, (h, t) in enumerate(steps):
             take_log(h, t)
-            if u > 0:
-                finish_z(*units[u - 1])
+            if i > 0:
+                make_z(*steps[i - 1])
             if h == 0:
-                copy_y(t)
-        finish_z(*units[-1])
+                fill_y_window(t)
+        make_z(*steps[-1])
+
+        z_dst = [z_grouped[h][:].rearrange("p (c i t) -> p c t i", i=LINE, t=PACK) for h in halves]
+        z_src = [z_tiles[h][:].rearrange("p t (c i) -> p c t i", i=LINE) for h in halves]
         nc.scalar.activation(z_dst[0], z_src[0], ACT.Copy)
         nc.vector.tensor_copy(z_dst[1], z_src[1])
         for h in halves:
             nc.vector.quantize_mx(
                 out=z_codes[:, half_cols[h]].bitcast(FP8X4), scales=z_scales[:, half_cols[h]], in_=z_grouped[h][:]
             )
+
         for t, cols, bank in s_pieces:
             product(bank, dealt_words, dealt_scales, t, z_codes, z_scales, cols)
 
-        out_rows = out.rearrange("(a t r) j -> t a r j", t=PACK, r=4)
-        last = PACK - 1
+        out_rows = out.rearrange("(a t r) j -> t a r j", t=PACK, r=LINE)
         identity = keep.tile([P, P], F32, name="identity")
         make_identity(nc, identity[:])
+        score, drop, rise, turned = (row_buffers(name, LAST) for name in ("score", "drop", "rise", "turned"))
+        result = row_buffers("result", PACK)
 
-        def tiles(name, count):
-            return [keep.tile([P, S], F32, name="%s%d" % (name, t)) for t in range(count)]
+        def fill_window(t, cols, bank):
+            nc.scalar.activation(window[t][:, cols], bank[:, cols], ACT.Copy, scale=-SCORE_SCALE)
+            if t < LAST:
+                nc.scalar.activation(score[t][:, cols], bank[:, cols], ACT.Copy, scale=SCORE_SCALE)
 
-        plain, drop, rise, least, turned = (tiles(name, last) for name in ("plain", "drop", "rise", "least", "turned"))
-        result = tiles("result", PACK)
-        gap4, gap5 = {}, {}
+        def make_drop(t):
+            nc.vector.tensor_tensor(drop[t][:], window[t][:].indirect(n3_list[:]), score[t][:], ALU.add)
 
-        def add_turned(bank, terms, h):
-            blocks = [(src, b) for src in terms for b in (2 * h, 2 * h + 1)]
-            for i, (src, b) in enumerate(blocks):
-                cols = slice(b * P, (b + 1) * P)
-                nc.tensor.matmul(
-                    bank[:, cols], src[:, cols], identity[:], start=(i == 0), stop=(i == len(blocks) - 1), is_transpose=True
-                )
-
-        def window(t, cols, bank):
-            nc.scalar.activation(first_window[t][:, cols], bank[:, cols], ACT.Copy, scale=-0.0625)
-            if t < last:
-                nc.scalar.activation(plain[t][:, cols], bank[:, cols], ACT.Copy, scale=0.0625)
-
-        def against3(t):
-            nc.vector.tensor_tensor(drop[t][:], first_window[t][:].indirect(n3_list[:]), plain[t][:], ALU.add)
-
-        def rectify(t):
+        def make_rise(t):
             nc.scalar.activation(rise[t][:], drop[t][:], ACT.Relu, scale=-1.0)
 
-        def against4(t):
-            gap4[t] = ring.tile([P, S], F32, name="gap4", bufs=2)
-            nc.vector.tensor_tensor(gap4[t][:], first_window[t][:].indirect(n4_list[:]), rise[t][:], ALU.add)
-
-        def against5(t):
-            gap5[t] = ring.tile([P, S], F32, name="gap5", bufs=1)
-            nc.vector.tensor_tensor(gap5[t][:], first_window[t][:].indirect(n5_list[:]), rise[t][:], ALU.add)
-
-        def smaller_gap(t):
-            nc.vector.tensor_tensor(least[t][:], gap4[t][:], gap5[t][:], ALU.min)
-            add_and_store(t, [plain[t], least[t]])
+        def add_transposed(bank, terms, h):
+            blocks = [(term, b) for term in terms for b in (2 * h, 2 * h + 1)]
+            for i, (term, b) in enumerate(blocks):
+                cols = slice(b * P, (b + 1) * P)
+                nc.tensor.matmul(
+                    bank[:, cols], term[:, cols], identity[:], start=(i == 0), stop=(i == len(blocks) - 1), is_transpose=True
+                )
 
         def add_and_store(t, terms):
             for h, cols in enumerate(half_cols):
-                add_turned(y_bank[h], terms, h)
+                add_transposed(y_bank[h], terms, h)
                 nc.scalar.copy(turned[t][:, cols], y_bank[h][:, cols])
             for h, cols in enumerate(half_cols):
-                add_turned(y_bank[2 + h], [turned[t]], h)
+                add_transposed(y_bank[2 + h], [turned[t]], h)
                 nc.scalar.copy(result[t][:, cols], y_bank[2 + h][:, cols])
-            nc.scalar.dma_start(out_rows[t], result[t][:])
+                nc.scalar.dma_start(out_rows[t][:, :, cols], result[t][:, cols])
 
-        for h in halves:
-            window(*s_pieces[h])
-        at4, excess, shortfall = tiles("first", 3)
-        step5 = drop[2]
-        nc.vector.tensor_copy(at4[:], first_window[0][:].indirect(n4_list[:]))
-        against3(0)
-        nc.vector.tensor_tensor(step5[:], first_window[0][:].indirect(n5_list[:]), at4[:], ALU.subtract)
-        window(*s_pieces[2])
-        rectify(0)
-        window(*s_pieces[3])
-        nc.scalar.activation(excess[:], step5[:], ACT.Relu, scale=-1.0)
+        first_half0, second_half0, piece1, piece2, piece3 = s_pieces
+        fill_window(*first_half0)
+        fill_window(*second_half0)
+        at_n4, excess, shortfall = row_buffers("tile0_", 3)
+        n5_less_n4 = drop[2]
+        nc.vector.tensor_copy(at_n4[:], window[0][:].indirect(n4_list[:]))
+        make_drop(0)
+        nc.vector.tensor_tensor(n5_less_n4[:], window[0][:].indirect(n5_list[:]), at_n4[:], ALU.subtract)
+        fill_window(*piece1)
+        make_rise(0)
+        fill_window(*piece2)
+        nc.scalar.activation(excess[:], n5_less_n4[:], ACT.Relu, scale=-1.0)
         nc.scalar.activation(shortfall[:], excess[:], ACT.Copy, scale=-1.0)
-        against3(1)
-        rectify(1)
-        window(*s_pieces[4])
-        against3(2)
-        rectify(2)
-        add_and_store(0, [plain[0], at4, rise[0], shortfall])
-        against4(1)
-        against5(1)
-        against4(2)
-        smaller_gap(1)
-        against5(2)
+        make_drop(1)
+        make_rise(1)
+        fill_window(*piece3)
+        make_drop(2)
+        make_rise(2)
+        add_and_store(0, [score[0], at_n4, rise[0], shortfall])
 
-        at3 = ring.tile([P, S], F32, name="gap4", bufs=2)
-        lower, end4, end5 = tiles("end", 3)
+        at_n3 = drop[1]
+        for h, t in enumerate((1, 2)):
+            gap4 = ring.tile([P, S], F32, name="gap4", bufs=2)
+            nc.vector.tensor_tensor(gap4[:], window[t][:].indirect(n4_list[:]), rise[t][:], ALU.add)
+            gap5 = ring.tile([P, S], F32, name="gap5", bufs=1)
+            nc.vector.tensor_tensor(gap5[:], window[t][:].indirect(n5_list[:]), rise[t][:], ALU.add)
+            nc.vector.tensor_copy(at_n3[:, half_cols[h]], window[LAST][:].indirect(n3_list[:, half_list[h]]))
+            least_gap = keep.tile([P, S], F32, name="least_gap%d" % t)
+            nc.vector.tensor_tensor(least_gap[:], gap4[:], gap5[:], ALU.min)
+            add_and_store(t, [score[t], least_gap])
 
-        def fetch3(h):
-            nc.vector.tensor_copy(at3[:, half_cols[h]], first_window[last][:].indirect(n3_list[:, half_list[h]]))
-
-        fetch3(0)
-        smaller_gap(2)
-        fetch3(1)
+        lower, last_gap4, last_gap5 = row_buffers("tile3_", 3)
         for cols in half_cols:
-            nc.vector.tensor_tensor(lower[:, cols], first_window[last][:, cols], at3[:, cols], ALU.min)
+            nc.vector.tensor_tensor(lower[:, cols], window[LAST][:, cols], at_n3[:, cols], ALU.min)
         for h, cols in enumerate(half_cols):
-            for dst, offsets in ((end4, n4_list), (end5, n5_list)):
+            for gap, offsets in ((last_gap4, n4_list), (last_gap5, n5_list)):
                 nc.vector.tensor_tensor(
-                    dst[:, cols], first_window[last][:].indirect(offsets[:, half_list[h]]), lower[:, cols], ALU.subtract
+                    gap[:, cols], window[LAST][:].indirect(offsets[:, half_list[h]]), lower[:, cols], ALU.subtract
                 )
         for cols in half_cols:
-            nc.vector.tensor_tensor(result[last][:, cols], end4[:, cols], end5[:, cols], ALU.min)
-            nc.sync.dma_start(out_rows[last][:, :, cols], result[last][:, cols])
+            nc.vector.tensor_tensor(result[LAST][:, cols], last_gap4[:, cols], last_gap5[:, cols], ALU.min)
+            nc.sync.dma_start(out_rows[LAST][:, :, cols], result[LAST][:, cols])

from contextlib import ExitStack

import concourse.mybir as mybir
from concourse.masks import make_identity

K, T, S, H, C = 512, 2048, 512, 512, 512
FLOPS = 2 * K * H * S + 2 * K * C * S

F32 = mybir.dt.float32
BF16 = mybir.dt.bfloat16
I32 = mybir.dt.int32
U32 = mybir.dt.uint32
U16 = mybir.dt.uint16
U8 = mybir.dt.uint8
FP8X4 = mybir.dt.float8_e4m3fn_x4
ALU = mybir.AluOpType
ACT = mybir.ActivationFunctionType

P = 128
PACK = 4
LAST = PACK - 1
HALF = S // 2
WINDOW = 2 * S
LIST_COLS = S // 16
LINE = 4
SCORE_SCALE = 0.0625


def tile_picked_candlsemix_none_p_kernel(
    tc, x_words, x_scales, w1, gs, offs, n1, n2, cand, n3, n4, n5, out
):
    nc = tc.nc
    row_tiles = range(PACK)
    halves = range(2)
    half_cols = [slice(h * HALF, (h + 1) * HALF) for h in halves]
    half_list = [slice(h * (LIST_COLS // 2), (h + 1) * (LIST_COLS // 2)) for h in halves]

    with ExitStack() as ctx:
        keep = ctx.enter_context(tc.tile_pool(name="keep", bufs=1))
        ring = ctx.enter_context(tc.tile_pool(name="ring", bufs=1))
        shared = ctx.enter_context(tc.tile_pool(name="shared", bufs=1))
        psum = ctx.enter_context(tc.psum_pool(name="psum", bufs=1))

        def load_list(name, dram):
            tile = keep.tile([P, LIST_COLS], U16, name=name)
            nc.sync.dma_start(tile[:], dram)
            return tile

        def row_buffers(name, count):
            return [keep.tile([P, S], F32, name="%s%d" % (name, i)) for i in range(count)]

        table_scales = keep.tile([P, T], U8, name="table_scales")
        nc.gpsimd.memset(table_scales[:, : T // 2].bitcast(I32), 0)
        nc.vector.memset(table_scales[:, T // 2 :].bitcast(I32), 0)
        offs_list = load_list("offs_list", offs)
        cand_list = load_list("cand_list", cand)
        for q in range(4):
            (nc.sync, nc.scalar)[q % 2].dma_start(
                table_scales[32 * q : 32 * q + 4, :].bitcast(I32),
                x_scales[0, 4 * q : 4 * q + 4, :].bitcast(I32),
            )
        w_rows = w1.rearrange("(p j) c -> p j c", j=PACK)
        w_raw = [keep.tile([P, PACK, H // 2], F32, name="w_raw%d" % h) for h in halves]
        for h in halves:
            nc.sync.dma_start(w_raw[h][:], w_rows[:, :, h * (H // 2) : (h + 1) * (H // 2)])
        table_words = keep.tile([P, T], U32, name="table_words")
        nc.sync.dma_start(
            table_words[:].bitcast(I32), x_words[0].rearrange("p n j -> p (n j)").bitcast(I32)
        )
        gain = keep.tile([P, PACK], F32, name="gain")
        nc.sync.dma_start(gain[:], gs.rearrange("(p t) o -> p (t o)", t=PACK))
        n1_list = load_list("n1_list", n1)
        n2_list = load_list("n2_list", n2)
        n3_list = load_list("n3_list", n3)
        n4_list = load_list("n4_list", n4)
        n5_list = load_list("n5_list", n5)

        window = [keep.tile([P, WINDOW], F32, name="window%d" % t) for t in row_tiles]
        y_window = [keep.tile([P, WINDOW], F32, name="y_window%d" % t) for t in row_tiles]
        for t in row_tiles:
            nc.vector.memset(window[t][:, S:], 0.0)

        tok_scales = keep.tile([P, S], U8, name="tok_scales", align_bytes=64)
        cand_scales = keep.tile([P, C], U8, name="cand_scales", align_bytes=64)
        nc.vector.tensor_copy(tok_scales[:], table_scales[:].indirect(offs_list[:]))
        nc.vector.tensor_copy(cand_scales[:], table_scales[:].indirect(cand_list[:]))
        dealt_scales = keep.tile([P, C], U8, name="dealt_scales", align_bytes=64)
        nc.vector.tensor_copy(
            dealt_scales[:].bitcast(I32).rearrange("p (t a) -> p a t", t=PACK),
            cand_scales[:].bitcast(I32).rearrange("p (a t) -> p a t", t=PACK),
        )

        w_grouped = shared.tile([P, PACK * P * PACK], BF16, name="w_grouped", align_bytes=64, offset=0)
        w_dealt = w_grouped[:].rearrange("p (t m j) -> p m j t", t=PACK, j=PACK)
        for h in halves:
            nc.scalar.activation(
                w_dealt[:, h * (P // 2) : (h + 1) * (P // 2)],
                w_raw[h][:].rearrange("p j (m t) -> p m j t", t=PACK),
                ACT.Copy,
            )
        w_codes = keep.tile([P, H], U32, name="w_codes", align_bytes=64)
        w_scales = keep.tile([P, H], U8, name="w_scales", align_bytes=64)
        y_bank = [psum.tile([P, S], F32, name="y_bank%d" % t) for t in row_tiles]
        s_bank = [psum.tile([P, S], F32, name="s_bank%d" % t) for t in row_tiles]
        nc.vector.quantize_mx(out=w_codes[:].bitcast(FP8X4), scales=w_scales[:], in_=w_grouped[:])

        tok_words = shared.tile([P, S], U32, name="tok_words", align_bytes=64, offset=0)
        for h in halves:
            nc.vector.tensor_copy(tok_words[:, half_cols[h]], table_words[:].indirect(offs_list[:, half_list[h]]))

        def product(bank, words, scales, t, moving_words, moving_scales, cols):
            rows = slice(t * P, (t + 1) * P)
            nc.tensor.matmul_mx(
                out=bank[:, cols],
                lhsT=words[:, rows].bitcast(FP8X4),
                lhsT_scale=scales[:, rows],
                rhs=moving_words[:, cols].bitcast(FP8X4),
                rhs_scale=moving_scales[:, cols],
                start=True,
                stop=True,
            )

        def pieces(banks, spare_bank):
            return [(0, half_cols[0], spare_bank), (0, half_cols[1], banks[0])] + [
                (t, slice(0, S), banks[t]) for t in range(1, PACK)
            ]

        y_pieces = pieces(y_bank, s_bank[0])
        s_pieces = pieces(s_bank, y_bank[0])
        for t, cols, bank in y_pieces:
            product(bank, w_codes, w_scales, t, tok_words, tok_scales, cols)

        dealt_words = shared.tile([P, C], U32, name="dealt_words", align_bytes=64, offset=4 * S)
        nc.vector.tensor_copy(
            dealt_words[:].rearrange("p (t a r) -> p a t r", t=PACK, r=LINE), table_words[:].indirect(cand_list[:])
        )

        sums = row_buffers("sums", PACK)
        for t, cols, bank in y_pieces:
            nc.scalar.activation(window[t][:, cols], bank[:, cols], ACT.Exp)

        def add_looked_up(t):
            nc.vector.tensor_tensor(sums[t][:], window[t][:].indirect(n1_list[:]), y_window[t][:, S:], ALU.add)

        for t in row_tiles:
            nc.vector.tensor_copy(y_window[t][:, S:], window[t][:, :S])
            if t > 0:
                add_looked_up(t - 1)
        add_looked_up(LAST)

        neg_gain = keep.tile([P, PACK], F32, name="neg_gain")
        nc.gpsimd.tensor_scalar(neg_gain[:], gain[:], -1.0, None, ALU.mult)
        logs = row_buffers("logs", PACK)
        weighted_logs = row_buffers("weighted_logs", PACK)
        z_tiles = [keep.tile([P, PACK, HALF], F32, name="z_tiles%d" % h) for h in halves]
        z_grouped = [keep.tile([P, HALF * PACK], BF16, name="z_grouped%d" % h, align_bytes=64) for h in halves]
        z_codes = keep.tile([P, S], U32, name="z_codes", align_bytes=64)
        z_scales = keep.tile([P, S], U8, name="z_scales", align_bytes=64)

        def fill_y_window(t):
            for piece_tile, cols, bank in y_pieces:
                if piece_tile == t:
                    nc.scalar.activation(y_window[t][:, cols], bank[:, cols], ACT.Copy, scale=neg_gain[:, t : t + 1])

        def take_log(h, t):
            nc.scalar.activation(logs[t][:, half_cols[h]], sums[t][:, half_cols[h]], ACT.Ln)

        def make_z(h, t):
            cols = half_cols[h]
            nc.scalar.activation(weighted_logs[t][:, cols], logs[t][:, cols], ACT.Copy, scale=gain[:, t : t + 1])
            nc.vector.tensor_tensor(
                z_tiles[h][:, t, :], y_window[t][:].indirect(n2_list[:, half_list[h]]), weighted_logs[t][:, cols], ALU.add
            )

        steps = [(h, t) for pair in ((0, 1), (2, 3)) for h in halves for t in pair]
        for i, (h, t) in enumerate(steps):
            take_log(h, t)
            if i > 0:
                make_z(*steps[i - 1])
            if h == 0:
                fill_y_window(t)
        make_z(*steps[-1])

        z_dst = [z_grouped[h][:].rearrange("p (c i t) -> p c t i", i=LINE, t=PACK) for h in halves]
        z_src = [z_tiles[h][:].rearrange("p t (c i) -> p c t i", i=LINE) for h in halves]
        nc.scalar.activation(z_dst[0], z_src[0], ACT.Copy)
        nc.vector.tensor_copy(z_dst[1], z_src[1])
        for h in halves:
            nc.vector.quantize_mx(
                out=z_codes[:, half_cols[h]].bitcast(FP8X4), scales=z_scales[:, half_cols[h]], in_=z_grouped[h][:]
            )

        for t, cols, bank in s_pieces:
            product(bank, dealt_words, dealt_scales, t, z_codes, z_scales, cols)

        out_rows = out.rearrange("(a t r) j -> t a r j", t=PACK, r=LINE)
        identity = keep.tile([P, P], F32, name="identity")
        make_identity(nc, identity[:])
        score, drop, rise, turned = (row_buffers(name, LAST) for name in ("score", "drop", "rise", "turned"))
        result = row_buffers("result", PACK)

        def fill_window(t, cols, bank):
            nc.scalar.activation(window[t][:, cols], bank[:, cols], ACT.Copy, scale=-SCORE_SCALE)
            if t < LAST:
                nc.scalar.activation(score[t][:, cols], bank[:, cols], ACT.Copy, scale=SCORE_SCALE)

        def make_drop(t):
            nc.vector.tensor_tensor(drop[t][:], window[t][:].indirect(n3_list[:]), score[t][:], ALU.add)

        def make_rise(t):
            nc.scalar.activation(rise[t][:], drop[t][:], ACT.Relu, scale=-1.0)

        def add_transposed(bank, terms, h):
            blocks = [(term, b) for term in terms for b in (2 * h, 2 * h + 1)]
            for i, (term, b) in enumerate(blocks):
                cols = slice(b * P, (b + 1) * P)
                nc.tensor.matmul(
                    bank[:, cols], term[:, cols], identity[:], start=(i == 0), stop=(i == len(blocks) - 1), is_transpose=True
                )

        def add_and_store(t, terms):
            for h, cols in enumerate(half_cols):
                add_transposed(y_bank[h], terms, h)
                nc.scalar.copy(turned[t][:, cols], y_bank[h][:, cols])
            for h, cols in enumerate(half_cols):
                add_transposed(y_bank[2 + h], [turned[t]], h)
                nc.scalar.copy(result[t][:, cols], y_bank[2 + h][:, cols])
                nc.scalar.dma_start(out_rows[t][:, :, cols], result[t][:, cols])

        first_half0, second_half0, piece1, piece2, piece3 = s_pieces
        fill_window(*first_half0)
        fill_window(*second_half0)
        at_n4, excess, shortfall = row_buffers("tile0_", 3)
        n5_less_n4 = drop[2]
        nc.vector.tensor_copy(at_n4[:], window[0][:].indirect(n4_list[:]))
        make_drop(0)
        nc.vector.tensor_tensor(n5_less_n4[:], window[0][:].indirect(n5_list[:]), at_n4[:], ALU.subtract)
        fill_window(*piece1)
        make_rise(0)
        fill_window(*piece2)
        nc.scalar.activation(excess[:], n5_less_n4[:], ACT.Relu, scale=-1.0)
        nc.scalar.activation(shortfall[:], excess[:], ACT.Copy, scale=-1.0)
        make_drop(1)
        make_rise(1)
        fill_window(*piece3)
        make_drop(2)
        make_rise(2)
        add_and_store(0, [score[0], at_n4, rise[0], shortfall])

        at_n3 = drop[1]
        for h, t in enumerate((1, 2)):
            gap4 = ring.tile([P, S], F32, name="gap4", bufs=2)
            nc.vector.tensor_tensor(gap4[:], window[t][:].indirect(n4_list[:]), rise[t][:], ALU.add)
            gap5 = ring.tile([P, S], F32, name="gap5", bufs=1)
            nc.vector.tensor_tensor(gap5[:], window[t][:].indirect(n5_list[:]), rise[t][:], ALU.add)
            nc.vector.tensor_copy(at_n3[:, half_cols[h]], window[LAST][:].indirect(n3_list[:, half_list[h]]))
            least_gap = keep.tile([P, S], F32, name="least_gap%d" % t)
            nc.vector.tensor_tensor(least_gap[:], gap4[:], gap5[:], ALU.min)
            add_and_store(t, [score[t], least_gap])

        lower, last_gap4, last_gap5 = row_buffers("tile3_", 3)
        for cols in half_cols:
            nc.vector.tensor_tensor(lower[:, cols], window[LAST][:, cols], at_n3[:, cols], ALU.min)
        for h, cols in enumerate(half_cols):
            for gap, offsets in ((last_gap4, n4_list), (last_gap5, n5_list)):
                nc.vector.tensor_tensor(
                    gap[:, cols], window[LAST][:].indirect(offsets[:, half_list[h]]), lower[:, cols], ALU.subtract
                )
        for cols in half_cols:
            nc.vector.tensor_tensor(result[LAST][:, cols], last_gap4[:, cols], last_gap5[:, cols], ALU.min)
            nc.sync.dma_start(out_rows[LAST][:, :, cols], result[LAST][:, cols])
